import numpy as np
import ml_dtypes


def mxq(x, axis, fmt="e4m3"):
    dtype, down = {"e4m3": (ml_dtypes.float8_e4m3fn, 7), "e5m2": (ml_dtypes.float8_e5m2, 14)}[fmt]
    v = np.moveaxis(np.asarray(x, np.float32).astype(ml_dtypes.bfloat16).astype(np.float64), axis, -1)
    blocks = v.reshape(v.shape[:-1] + (-1, 32))
    amax = np.abs(blocks).max(-1, keepdims=True)
    byte = np.maximum(np.where(amax > 0, np.frexp(amax)[1] - 1 + 127, 0) - down, 1)
    scale = np.exp2(byte - 127.0)
    codes = (blocks / scale).astype(np.float32).astype(dtype).astype(np.float64)
    return np.moveaxis((codes * scale).reshape(v.shape), -1, axis)


WIDE = False


def mx_kscale(k):
    if not WIDE:
        return np.ones(k)
    levels = np.array([10, -10, 5, -5, 0])
    if k % 512:
        return np.exp2(np.random.permutation(np.resize(levels, k // 32))).repeat(32)
    a = np.empty((k // 512, 16))
    for p in range(k // 512):
        a[p, :8] = np.random.permutation(np.resize(levels, 8))
        for g in range(8):
            far = levels[np.abs(levels - a[p, g]) >= 10]
            a[p, g + 8] = far[np.random.randint(len(far))]
    return np.exp2(a.ravel()).repeat(32)


def f64(x):
    return np.asarray(x).astype(np.float64)


def striped8(idx):
    return np.asarray(idx).reshape(8, -1, 16).transpose(0, 2, 1).reshape(128, -1).astype(np.uint16)


def unstriped8(offs):
    return offs.reshape(8, 16, -1).transpose(0, 2, 1).reshape(8, -1).astype(np.int64)


def pick8(x, idx, run):
    r = np.arange(len(x))
    return x[r[:, None], idx[r % (8 * run) // run]]


E2M1 = np.array([0.0, 0.5, 1.0, 1.5, 2.0, 3.0, 4.0, 6.0, -0.0, -0.5, -1.0, -1.5, -2.0, -3.0, -4.0, -6.0])


def pack_weight(w, fmt):
    k, n = w.shape
    w = f64(np.asarray(w, np.float32).astype(ml_dtypes.bfloat16)).reshape(k // 32, 32, n)
    amax = np.abs(w).max(1)
    if fmt == "e4m3":
        byte = np.frexp(amax)[1] - 1 + 127 - 7
    else:
        mant, ex = np.frexp(amax / 6.0)
        byte = np.where(mant > 0.5, ex, ex - 1) + 127
    byte = np.clip(np.where(amax > 0, byte, 1), 1, 254)
    scaled = (w * np.exp2(127.0 - byte)[:, None, :]).reshape(k, n).astype(np.float32)
    by_word = np.ascontiguousarray(scaled.reshape(k // 512, 128, 4, n).transpose(0, 1, 3, 2))
    if fmt == "e4m3":
        words = by_word.astype(ml_dtypes.float8_e4m3fn).view(np.uint8)
    else:
        c = by_word.astype(ml_dtypes.float4_e2m1fn).view(np.uint8) & 0xF
        words = (c[..., 0::2] | (c[..., 1::2] << 4)).reshape(k // 512, 128, 2 * n)
    return np.ascontiguousarray(words), np.ascontiguousarray(byte.astype(np.uint8).reshape(k // 512, 16, n))


def unpack_weight(words, scales, fmt):
    g, _, n = scales.shape
    words = np.ascontiguousarray(words).reshape(g, 128, n, -1)
    if fmt == "e4m3":
        vals = words.view(ml_dtypes.float8_e4m3fn).astype(np.float64)
    else:
        nib = np.empty((g, 128, n, 4), np.uint8)
        nib[..., 0::2] = words & 0xF
        nib[..., 1::2] = words >> 4
        vals = E2M1[nib]
    vals = vals * np.repeat(np.exp2(scales.astype(np.float64) - 127.0), 8, axis=1)[..., None]
    return vals.transpose(0, 1, 3, 2).reshape(g * 512, n)


D, T, U, I, J, Q = 512, 1024, 1024, 512, 256, 128


def setup_inputs():
    n = np.random.standard_normal
    idx = np.stack([np.random.permutation(T)[:I] for _ in range(8)])
    idx2 = np.stack([np.random.permutation(U)[:I] for _ in range(8)])
    idx3 = np.stack([np.random.permutation(I)[:J] for _ in range(8)])
    idx4 = np.stack([np.random.permutation(I)[:J] for _ in range(8)])
    idx5 = np.stack([np.random.permutation(T)[:J] for _ in range(8)])
    idx6 = np.stack([np.random.permutation(T)[:I] for _ in range(8)])
    fd = mx_kscale(D)
    cachep = pack_weight(n((D, T)) / fd[:, None], "e4m3")
    draftp = pack_weight(n((D, U)) / fd[:, None], "e2m1")
    return {
        "query": (n((D, Q)) * 1.0 / np.sqrt(D) * fd[:, None]).astype(np.float32),
        "cache_words": cachep[0],
        "cache_scales": cachep[1],
        "draft_words": draftp[0],
        "draft_scales": draftp[1],
        "offs": striped8(idx),
        "offs2": striped8(idx2),
        "offs3": striped8(idx3),
        "offs4": striped8(idx4),
        "offs5": striped8(idx5),
        "offs6": striped8(idx6),
    }


def reference(query, cache_words, cache_scales, draft_words, draft_scales, offs, offs2, offs3, offs4, offs5, offs6):
    idx = unstriped8(offs)
    idx2 = unstriped8(offs2)
    idx3 = unstriped8(offs3)
    idx4 = unstriped8(offs4)
    idx5 = unstriped8(offs5)
    idx6 = unstriped8(offs6)
    cacheu = unpack_weight(cache_words, cache_scales, "e4m3")
    draftu = unpack_weight(draft_words, draft_scales, "e2m1")
    queryq = mxq(f64(query), 0, "e4m3")
    a = queryq.T @ cacheu
    b = queryq.T @ draftu
    w = pick8(a, idx, 16) - pick8(b, idx2, 16)
    p1 = np.maximum(pick8(w, idx3, 16), pick8(w, idx4, 16))
    f1 = np.zeros((Q, T))
    f1[np.arange(Q)[:, None], idx5[np.arange(Q) % 128 // 16]] = p1
    aa = a - f1
    y = pick8(aa, idx6, 16) + w
    return y

@@ -1,0 +1,134 @@
+from contextlib import ExitStack
+
+import concourse.mybir as mybir
+
+D, T, U, I, J, Q = 512, 1024, 1024, 512, 256, 128
+FLOPS = 2 * D * Q * (T + U)
+
+F32 = mybir.dt.float32
+BF16 = mybir.dt.bfloat16
+I32 = mybir.dt.int32
+U32 = mybir.dt.uint32
+U16 = mybir.dt.uint16
+U8 = mybir.dt.uint8
+FP8X4 = mybir.dt.float8_e4m3fn_x4
+FP4X4 = mybir.dt.float4_e2m1fn_x4
+COPY = mybir.ActivationFunctionType.Copy
+ADD = mybir.AluOpType.add
+SUB = mybir.AluOpType.subtract
+MAX = mybir.AluOpType.max
+
+P = 128
+PACK = 4
+LANES = 16
+PIECE = 256
+CACHE_ROW = 4
+
+
+def tile_attend_bestslots_two_kernel(tc, query, cache_words, cache_scales, draft_words, draft_scales,
+                                      offs, offs2, offs3, offs4, offs5, offs6, out):
+    nc = tc.nc
+    with ExitStack() as ctx:
+        sb = ctx.enter_context(tc.tile_pool(name="sb", bufs=1))
+        psum = ctx.enter_context(tc.psum_pool(name="psum", bufs=1))
+
+        planes = sb.tile([P, 2 * T], U8, align_bytes=64)
+        planes_i = planes[:].bitcast(I32)
+        half = T // 4
+        nc.vector.memset(planes_i, 0)
+
+        q_raw = sb.tile([P, PACK, Q], F32)
+        nc.sync.dma_start(q_raw[:], query.rearrange("(p t) q -> p t q", t=PACK))
+        for scales, row in ((draft_scales, 0), (cache_scales, CACHE_ROW)):
+            rows = scales[0].bitcast(I32)
+            for pair in range(2):
+                first = 64 * pair + row
+                nc.scalar.dma_start(
+                    planes_i[first : first + 4, :].rearrange("r (h n) -> r h n", h=2),
+                    rows[8 * pair : 8 * pair + 8, :].rearrange("(h r) n -> r h n", h=2),
+                )
+        draft_sb = sb.tile([P, 2 * U], U8, align_bytes=64)
+        nc.sync.dma_start(draft_sb[:].bitcast(I32), draft_words[0].bitcast(I32))
+        cache_bytes = cache_words[0].rearrange("p n t -> p (n t)")
+        cache_sb = []
+        for h in range(2):
+            words = sb.tile([P, T // 2], U32, name="cache_sb%d" % h, align_bytes=64)
+            nc.sync.dma_start(words[:].bitcast(I32), cache_bytes[:, 2 * T * h : 2 * T * (h + 1)].bitcast(I32))
+            cache_sb.append(words)
+
+        lists = {}
+        for name, src, n in (("offs2", offs2, I), ("offs", offs, I), ("offs3", offs3, J), ("offs4", offs4, J),
+                             ("offs5", offs5, J), ("offs6", offs6, I)):
+            lists[name] = sb.tile([P, n // LANES], U16, name=name)
+            nc.sync.dma_start(lists[name][:], src)
+
+        def part(name, lo, hi):
+            return lists[name][:, lo // LANES : hi // LANES]
+
+        f1 = sb.tile([P, T], F32)
+        nc.vector.memset(f1[:], 0.0)
+
+        for pair in range(2):
+            nc.vector.tensor_copy(planes_i[64 * pair + 32 : 64 * pair + 64, 0:half],
+                                  planes_i[64 * pair : 64 * pair + 32, half : 2 * half])
+
+        q_bf = sb.tile([P, Q, PACK], BF16, align_bytes=64)
+        q_view = q_raw[:].rearrange("p t q -> p q t")
+        nc.vector.tensor_copy(q_bf[:, 0 : Q // 2, :], q_view[:, 0 : Q // 2, :])
+        nc.scalar.activation(q_bf[:, Q // 2 : Q, :], q_view[:, Q // 2 : Q, :], COPY)
+        q_codes = sb.tile([P, Q], U32, align_bytes=64)
+        q_scales = sb.tile([P, Q], U8, align_bytes=64)
+        nc.vector.quantize_mx(out=q_codes[:].bitcast(FP8X4), scales=q_scales[:],
+                              in_=q_bf[:].rearrange("p q t -> p (q t)"))
+
+        b_sb = sb.tile([P, U], F32)
+        for c in range(U // PIECE):
+            cols = slice(c * PIECE, (c + 1) * PIECE)
+            bank = psum.tile([P, PIECE], F32, name="b_bank%d" % c)
+            nc.tensor.matmul_mx(out=bank[:], lhsT=q_codes[:].bitcast(FP8X4), lhsT_scale=q_scales[:],
+                                rhs=draft_sb[:, 2 * cols.start : 2 * cols.stop].bitcast(FP4X4),
+                                rhs_scale=planes[:, cols], start=True, stop=True)
+            if c % 2 == 0:
+                nc.scalar.copy(b_sb[:, cols], bank[:])
+            else:
+                nc.vector.tensor_copy(b_sb[:, cols], bank[:])
+        gb = sb.tile([P, I], F32)
+        nc.scalar.activation(gb[:], b_sb[:].indirect(lists["offs2"][:]), COPY)
+
+        a_sb = sb.tile([P, T], F32)
+        for c in range(T // PIECE):
+            cols = slice(c * PIECE, (c + 1) * PIECE)
+            bank = psum.tile([P, PIECE], F32, name="a_bank%d" % c)
+            inner = (c % 2) * PIECE
+            nc.tensor.matmul_mx(out=bank[:], lhsT=q_codes[:].bitcast(FP8X4), lhsT_scale=q_scales[:],
+                                rhs=cache_sb[c // 2][:, inner : inner + PIECE].bitcast(FP8X4),
+                                rhs_scale=planes[CACHE_ROW:P, cols], start=True, stop=True)
+            nc.vector.tensor_copy(a_sb[:, cols], bank[:])
+
+        w = sb.tile([P, I], F32)
+        ga = sb.tile([P, I // 2], F32)
+        nc.vector.tensor_tensor(w[:, 0 : I // 2], a_sb[:].indirect(part("offs", 0, I // 2)), gb[:, 0 : I // 2], SUB)
+        nc.scalar.activation(ga[:], a_sb[:].indirect(part("offs", I // 2, I)), COPY)
+        nc.vector.tensor_tensor(w[:, I // 2 : I], ga[:], gb[:, I // 2 : I], SUB)
+
+        for h in range(2):
+            lo, hi = h * J // 2, (h + 1) * J // 2
+            g3 = sb.tile([P, J // 2], F32, name="g3_%d" % h)
+            g4 = sb.tile([P, J // 2], F32, name="g4_%d" % h)
+            p1 = sb.tile([P, J // 2], F32, name="p1_%d" % h)
+            nc.vector.tensor_copy(g3[:], w[:].indirect(part("offs3", lo, hi)))
+            nc.scalar.activation(g4[:], w[:].indirect(part("offs4", lo, hi)), COPY)
+            nc.vector.tensor_tensor(p1[:], g3[:], g4[:], MAX)
+            nc.scalar.activation(f1[:].indirect(part("offs5", lo, hi)), p1[:], COPY)
+
+        aa = sb.tile([P, T], F32)
+        nc.vector.tensor_tensor(aa[:], a_sb[:], f1[:], SUB)
+
+        y0 = sb.tile([P, I // 2], F32)
+        nc.vector.tensor_tensor(y0[:], aa[:].indirect(part("offs6", 0, I // 2)), w[:, 0 : I // 2], ADD)
+        nc.sync.dma_start(out[:, 0 : I // 2], y0[:])
+        gaa = sb.tile([P, I // 2], F32)
+        nc.scalar.activation(gaa[:], aa[:].indirect(part("offs6", I // 2, I)), COPY)
+        y1 = sb.tile([P, I // 2], F32)
+        nc.vector.tensor_tensor(y1[:], gaa[:], w[:, I // 2 : I], ADD)
+        nc.sync.dma_start(out[:, I // 2 : I], y1[:])

@@ -22,7 +22,6 @@ P = 128
 PACK = 4
 LANES = 16
 PIECE = 256
-CACHE_ROW = 4
 
 
 def tile_attend_bestslots_two_kernel(tc, query, cache_words, cache_scales, draft_words, draft_scales,
@@ -32,21 +31,28 @@ def tile_attend_bestslots_two_kernel(tc, query, cache_words, cache_scales, draft
         sb = ctx.enter_context(tc.tile_pool(name="sb", bufs=1))
         psum = ctx.enter_context(tc.psum_pool(name="psum", bufs=1))
 
-        planes = sb.tile([P, 2 * T], U8, align_bytes=64)
-        planes_i = planes[:].bitcast(I32)
         half = T // 4
-        nc.vector.memset(planes_i, 0)
+
+        def load_scales(scales, name):
+            plane = sb.tile([P, 2 * T], U8, name=name, align_bytes=64)
+            rows = scales[0].bitcast(I32)
+            for pair in range(2):
+                nc.sync.dma_start(
+                    plane[:].bitcast(I32)[64 * pair : 64 * pair + 4, :].rearrange("r (h n) -> r h n", h=2),
+                    rows[8 * pair : 8 * pair + 8, :].rearrange("(h r) n -> r h n", h=2),
+                )
+            return plane
+
+        def spread_scales(plane):
+            words = plane[:].bitcast(I32)
+            for pair in range(2):
+                nc.vector.tensor_copy(words[64 * pair + 32 : 64 * pair + 36, 0:half],
+                                      words[64 * pair : 64 * pair + 4, half : 2 * half])
 
         q_raw = sb.tile([P, PACK, Q], F32)
         nc.sync.dma_start(q_raw[:], query.rearrange("(p t) q -> p t q", t=PACK))
-        for scales, row in ((draft_scales, 0), (cache_scales, CACHE_ROW)):
-            rows = scales[0].bitcast(I32)
-            for pair in range(2):
-                first = 64 * pair + row
-                nc.scalar.dma_start(
-                    planes_i[first : first + 4, :].rearrange("r (h n) -> r h n", h=2),
-                    rows[8 * pair : 8 * pair + 8, :].rearrange("(h r) n -> r h n", h=2),
-                )
+        draft_plane = load_scales(draft_scales, "draft_plane")
+        cache_plane = load_scales(cache_scales, "cache_plane")
         draft_sb = sb.tile([P, 2 * U], U8, align_bytes=64)
         nc.sync.dma_start(draft_sb[:].bitcast(I32), draft_words[0].bitcast(I32))
         cache_bytes = cache_words[0].rearrange("p n t -> p (n t)")
@@ -68,9 +74,7 @@ def tile_attend_bestslots_two_kernel(tc, query, cache_words, cache_scales, draft
         f1 = sb.tile([P, T], F32)
         nc.vector.memset(f1[:], 0.0)
 
-        for pair in range(2):
-            nc.vector.tensor_copy(planes_i[64 * pair + 32 : 64 * pair + 64, 0:half],
-                                  planes_i[64 * pair : 64 * pair + 32, half : 2 * half])
+        spread_scales(draft_plane)
 
         q_bf = sb.tile([P, Q, PACK], BF16, align_bytes=64)
         q_view = q_raw[:].rearrange("p t q -> p q t")
@@ -81,29 +85,37 @@ def tile_attend_bestslots_two_kernel(tc, query, cache_words, cache_scales, draft
         nc.vector.quantize_mx(out=q_codes[:].bitcast(FP8X4), scales=q_scales[:],
                               in_=q_bf[:].rearrange("p q t -> p (q t)"))
 
+        spread_scales(cache_plane)
+
         b_sb = sb.tile([P, U], F32)
         for c in range(U // PIECE):
             cols = slice(c * PIECE, (c + 1) * PIECE)
             bank = psum.tile([P, PIECE], F32, name="b_bank%d" % c)
             nc.tensor.matmul_mx(out=bank[:], lhsT=q_codes[:].bitcast(FP8X4), lhsT_scale=q_scales[:],
                                 rhs=draft_sb[:, 2 * cols.start : 2 * cols.stop].bitcast(FP4X4),
-                                rhs_scale=planes[:, cols], start=True, stop=True)
+                                rhs_scale=draft_plane[:, cols], start=True, stop=True)
             if c % 2 == 0:
                 nc.scalar.copy(b_sb[:, cols], bank[:])
             else:
                 nc.vector.tensor_copy(b_sb[:, cols], bank[:])
         gb = sb.tile([P, I], F32)
-        nc.scalar.activation(gb[:], b_sb[:].indirect(lists["offs2"][:]), COPY)
+        for lo in (0, I // 2):
+            nc.scalar.activation(gb[:, lo : lo + I // 2], b_sb[:].indirect(part("offs2", lo, lo + I // 2)), COPY)
 
         a_sb = sb.tile([P, T], F32)
+        a_banks = []
         for c in range(T // PIECE):
             cols = slice(c * PIECE, (c + 1) * PIECE)
             bank = psum.tile([P, PIECE], F32, name="a_bank%d" % c)
             inner = (c % 2) * PIECE
             nc.tensor.matmul_mx(out=bank[:], lhsT=q_codes[:].bitcast(FP8X4), lhsT_scale=q_scales[:],
                                 rhs=cache_sb[c // 2][:, inner : inner + PIECE].bitcast(FP8X4),
-                                rhs_scale=planes[CACHE_ROW:P, cols], start=True, stop=True)
-            nc.vector.tensor_copy(a_sb[:, cols], bank[:])
+                                rhs_scale=cache_plane[:, cols], start=True, stop=True)
+            a_banks.append(bank)
+            if c == 0:
+                nc.scalar.copy(a_sb[:, cols], bank[:])
+            else:
+                nc.vector.tensor_copy(a_sb[:, cols], bank[:])
 
         w = sb.tile([P, I], F32)
         ga = sb.tile([P, I // 2], F32)
@@ -122,7 +134,11 @@ def tile_attend_bestslots_two_kernel(tc, query, cache_words, cache_scales, draft
             nc.scalar.activation(f1[:].indirect(part("offs5", lo, hi)), p1[:], COPY)
 
         aa = sb.tile([P, T], F32)
-        nc.vector.tensor_tensor(aa[:], a_sb[:], f1[:], SUB)
+        last = slice(T - PIECE, T)
+        nc.gpsimd.tensor_tensor(aa[:, last], a_sb[:, last], f1[:, last], SUB)
+        for c in range(T // PIECE - 1):
+            cols = slice(c * PIECE, (c + 1) * PIECE)
+            nc.vector.tensor_tensor(aa[:, cols], a_banks[c][:], f1[:, cols], SUB)
 
         y0 = sb.tile([P, I // 2], F32)
         nc.vector.tensor_tensor(y0[:], aa[:].indirect(part("offs6", 0, I // 2)), w[:, 0 : I // 2], ADD)

@@ -52,9 +52,9 @@ def tile_attend_bestslots_two_kernel(tc, query, cache_words, cache_scales, draft
         q_raw = sb.tile([P, PACK, Q], F32)
         nc.sync.dma_start(q_raw[:], query.rearrange("(p t) q -> p t q", t=PACK))
         draft_plane = load_scales(draft_scales, "draft_plane")
-        cache_plane = load_scales(cache_scales, "cache_plane")
         draft_sb = sb.tile([P, 2 * U], U8, align_bytes=64)
         nc.sync.dma_start(draft_sb[:].bitcast(I32), draft_words[0].bitcast(I32))
+        cache_plane = load_scales(cache_scales, "cache_plane")
         cache_bytes = cache_words[0].rearrange("p n t -> p (n t)")
         cache_sb = []
         for h in range(2):
@@ -94,10 +94,7 @@ def tile_attend_bestslots_two_kernel(tc, query, cache_words, cache_scales, draft
             nc.tensor.matmul_mx(out=bank[:], lhsT=q_codes[:].bitcast(FP8X4), lhsT_scale=q_scales[:],
                                 rhs=draft_sb[:, 2 * cols.start : 2 * cols.stop].bitcast(FP4X4),
                                 rhs_scale=draft_plane[:, cols], start=True, stop=True)
-            if c % 2 == 0:
-                nc.scalar.copy(b_sb[:, cols], bank[:])
-            else:
-                nc.vector.tensor_copy(b_sb[:, cols], bank[:])
+            nc.scalar.copy(b_sb[:, cols], bank[:])
         gb = sb.tile([P, I], F32)
         for lo in (0, I // 2):
             nc.scalar.activation(gb[:, lo : lo + I // 2], b_sb[:].indirect(part("offs2", lo, lo + I // 2)), COPY)
@@ -112,16 +109,12 @@ def tile_attend_bestslots_two_kernel(tc, query, cache_words, cache_scales, draft
                                 rhs=cache_sb[c // 2][:, inner : inner + PIECE].bitcast(FP8X4),
                                 rhs_scale=cache_plane[:, cols], start=True, stop=True)
             a_banks.append(bank)
-            if c == 0:
-                nc.scalar.copy(a_sb[:, cols], bank[:])
-            else:
-                nc.vector.tensor_copy(a_sb[:, cols], bank[:])
+            nc.vector.tensor_copy(a_sb[:, cols], bank[:])
 
         w = sb.tile([P, I], F32)
-        ga = sb.tile([P, I // 2], F32)
-        nc.vector.tensor_tensor(w[:, 0 : I // 2], a_sb[:].indirect(part("offs", 0, I // 2)), gb[:, 0 : I // 2], SUB)
-        nc.scalar.activation(ga[:], a_sb[:].indirect(part("offs", I // 2, I)), COPY)
-        nc.vector.tensor_tensor(w[:, I // 2 : I], ga[:], gb[:, I // 2 : I], SUB)
+        for lo in (0, I // 2):
+            hi = lo + I // 2
+            nc.vector.tensor_tensor(w[:, lo:hi], a_sb[:].indirect(part("offs", lo, hi)), gb[:, lo:hi], SUB)
 
         for h in range(2):
             lo, hi = h * J // 2, (h + 1) * J // 2
@@ -140,11 +133,8 @@ def tile_attend_bestslots_two_kernel(tc, query, cache_words, cache_scales, draft
             cols = slice(c * PIECE, (c + 1) * PIECE)
             nc.vector.tensor_tensor(aa[:, cols], a_banks[c][:], f1[:, cols], SUB)
 
-        y0 = sb.tile([P, I // 2], F32)
-        nc.vector.tensor_tensor(y0[:], aa[:].indirect(part("offs6", 0, I // 2)), w[:, 0 : I // 2], ADD)
-        nc.sync.dma_start(out[:, 0 : I // 2], y0[:])
-        gaa = sb.tile([P, I // 2], F32)
-        nc.scalar.activation(gaa[:], aa[:].indirect(part("offs6", I // 2, I)), COPY)
-        y1 = sb.tile([P, I // 2], F32)
-        nc.vector.tensor_tensor(y1[:], gaa[:], w[:, I // 2 : I], ADD)
-        nc.sync.dma_start(out[:, I // 2 : I], y1[:])
+        for lo in (0, I // 2):
+            hi = lo + I // 2
+            y = sb.tile([P, I // 2], F32, name="y%d" % lo)
+            nc.vector.tensor_tensor(y[:], aa[:].indirect(part("offs6", lo, hi)), w[:, lo:hi], ADD)
+            nc.sync.dma_start(out[:, lo:hi], y[:])

@@ -33,34 +33,24 @@ def tile_attend_bestslots_two_kernel(tc, query, cache_words, cache_scales, draft
 
         half = T // 4
 
-        def load_scales(scales, name):
-            plane = sb.tile([P, 2 * T], U8, name=name, align_bytes=64)
-            rows = scales[0].bitcast(I32)
-            for pair in range(2):
-                nc.sync.dma_start(
-                    plane[:].bitcast(I32)[64 * pair : 64 * pair + 4, :].rearrange("r (h n) -> r h n", h=2),
-                    rows[8 * pair : 8 * pair + 8, :].rearrange("(h r) n -> r h n", h=2),
-                )
-            return plane
-
-        def spread_scales(plane):
-            words = plane[:].bitcast(I32)
-            for pair in range(2):
-                nc.vector.tensor_copy(words[64 * pair + 32 : 64 * pair + 36, 0:half],
-                                      words[64 * pair : 64 * pair + 4, half : 2 * half])
-
         q_raw = sb.tile([P, PACK, Q], F32)
         nc.sync.dma_start(q_raw[:], query.rearrange("(p t) q -> p t q", t=PACK))
-        draft_plane = load_scales(draft_scales, "draft_plane")
+        draft_plane = sb.tile([P, U], U8, align_bytes=64)
+        draft_rows = draft_scales[0].bitcast(I32).rearrange("(g r) n -> r g n", r=4)
+        for r in range(4):
+            nc.sync.dma_start(draft_plane[:].bitcast(I32)[r:P:32, :], draft_rows[r])
         draft_sb = sb.tile([P, 2 * U], U8, align_bytes=64)
         nc.sync.dma_start(draft_sb[:].bitcast(I32), draft_words[0].bitcast(I32))
-        cache_plane = load_scales(cache_scales, "cache_plane")
+        cache_plane = sb.tile([P, 4 * T], U8, align_bytes=64)
+        cache_plane_i = cache_plane[:].bitcast(I32)
+        nc.sync.dma_start(cache_plane_i[0:4, :].rearrange("r (g n) -> r g n", g=4),
+                          cache_scales[0].bitcast(I32).rearrange("(g r) n -> r g n", r=4))
         cache_bytes = cache_words[0].rearrange("p n t -> p (n t)")
         cache_sb = []
-        for h in range(2):
-            words = sb.tile([P, T // 2], U32, name="cache_sb%d" % h, align_bytes=64)
-            nc.sync.dma_start(words[:].bitcast(I32), cache_bytes[:, 2 * T * h : 2 * T * (h + 1)].bitcast(I32))
-            cache_sb.append(words)
+        for lo, hi in ((0, T - PIECE), (T - PIECE, T)):
+            words = sb.tile([P, hi - lo], U32, name="cache_sb%d" % lo, align_bytes=64)
+            nc.sync.dma_start(words[:].bitcast(I32), cache_bytes[:, PACK * lo : PACK * hi].bitcast(I32))
+            cache_sb.extend([words[:, c : c + PIECE] for c in range(0, hi - lo, PIECE)])
 
         lists = {}
         for name, src, n in (("offs2", offs2, I), ("offs", offs, I), ("offs3", offs3, J), ("offs4", offs4, J),
@@ -74,18 +64,17 @@ def tile_attend_bestslots_two_kernel(tc, query, cache_words, cache_scales, draft
         f1 = sb.tile([P, T], F32)
         nc.vector.memset(f1[:], 0.0)
 
-        spread_scales(draft_plane)
-
         q_bf = sb.tile([P, Q, PACK], BF16, align_bytes=64)
         q_view = q_raw[:].rearrange("p t q -> p q t")
-        nc.vector.tensor_copy(q_bf[:, 0 : Q // 2, :], q_view[:, 0 : Q // 2, :])
-        nc.scalar.activation(q_bf[:, Q // 2 : Q, :], q_view[:, Q // 2 : Q, :], COPY)
+        nc.vector.tensor_copy(q_bf[:, 0:88, :], q_view[:, 0:88, :])
+        nc.scalar.activation(q_bf[:, 88:Q, :], q_view[:, 88:Q, :], COPY)
         q_codes = sb.tile([P, Q], U32, align_bytes=64)
         q_scales = sb.tile([P, Q], U8, align_bytes=64)
         nc.vector.quantize_mx(out=q_codes[:].bitcast(FP8X4), scales=q_scales[:],
                               in_=q_bf[:].rearrange("p q t -> p (q t)"))
 
-        spread_scales(cache_plane)
+        for g in range(1, 4):
+            nc.vector.tensor_copy(cache_plane_i[32 * g : 32 * g + 4, 0:half], cache_plane_i[0:4, g * half : (g + 1) * half])
 
         b_sb = sb.tile([P, U], F32)
         for c in range(U // PIECE):
@@ -104,9 +93,8 @@ def tile_attend_bestslots_two_kernel(tc, query, cache_words, cache_scales, draft
         for c in range(T // PIECE):
             cols = slice(c * PIECE, (c + 1) * PIECE)
             bank = psum.tile([P, PIECE], F32, name="a_bank%d" % c)
-            inner = (c % 2) * PIECE
             nc.tensor.matmul_mx(out=bank[:], lhsT=q_codes[:].bitcast(FP8X4), lhsT_scale=q_scales[:],
-                                rhs=cache_sb[c // 2][:, inner : inner + PIECE].bitcast(FP8X4),
+                                rhs=cache_sb[c].bitcast(FP8X4),
                                 rhs_scale=cache_plane[:, cols], start=True, stop=True)
             a_banks.append(bank)
             nc.vector.tensor_copy(a_sb[:, cols], bank[:])

from contextlib import ExitStack

import concourse.mybir as mybir

D, T, U, I, J, Q = 512, 1024, 1024, 512, 256, 128
FLOPS = 2 * D * Q * (T + U)

F32 = mybir.dt.float32
BF16 = mybir.dt.bfloat16
I32 = mybir.dt.int32
U32 = mybir.dt.uint32
U16 = mybir.dt.uint16
U8 = mybir.dt.uint8
FP8X4 = mybir.dt.float8_e4m3fn_x4
FP4X4 = mybir.dt.float4_e2m1fn_x4
COPY = mybir.ActivationFunctionType.Copy
ADD = mybir.AluOpType.add
SUB = mybir.AluOpType.subtract
MAX = mybir.AluOpType.max

P = 128
PACK = 4
LANES = 16
PIECE = 256


def tile_attend_bestslots_two_kernel(tc, query, cache_words, cache_scales, draft_words, draft_scales,
                                      offs, offs2, offs3, offs4, offs5, offs6, out):
    nc = tc.nc
    with ExitStack() as ctx:
        sb = ctx.enter_context(tc.tile_pool(name="sb", bufs=1))
        psum = ctx.enter_context(tc.psum_pool(name="psum", bufs=1))

        half = T // 4

        q_raw = sb.tile([P, PACK, Q], F32)
        nc.sync.dma_start(q_raw[:], query.rearrange("(p t) q -> p t q", t=PACK))
        draft_plane = sb.tile([P, U], U8, align_bytes=64)
        draft_rows = draft_scales[0].bitcast(I32).rearrange("(g r) n -> r g n", r=4)
        for r in range(4):
            nc.sync.dma_start(draft_plane[:].bitcast(I32)[r:P:32, :], draft_rows[r])
        draft_sb = sb.tile([P, 2 * U], U8, align_bytes=64)
        nc.sync.dma_start(draft_sb[:].bitcast(I32), draft_words[0].bitcast(I32))
        cache_plane = sb.tile([P, 4 * T], U8, align_bytes=64)
        cache_plane_i = cache_plane[:].bitcast(I32)
        nc.sync.dma_start(cache_plane_i[0:4, :].rearrange("r (g n) -> r g n", g=4),
                          cache_scales[0].bitcast(I32).rearrange("(g r) n -> r g n", r=4))
        cache_bytes = cache_words[0].rearrange("p n t -> p (n t)")
        cache_sb = []
        for lo, hi in ((0, T - PIECE), (T - PIECE, T)):
            words = sb.tile([P, hi - lo], U32, name="cache_sb%d" % lo, align_bytes=64)
            nc.sync.dma_start(words[:].bitcast(I32), cache_bytes[:, PACK * lo : PACK * hi].bitcast(I32))
            cache_sb.extend([words[:, c : c + PIECE] for c in range(0, hi - lo, PIECE)])

        lists = {}
        for name, src, n in (("offs2", offs2, I), ("offs", offs, I), ("offs3", offs3, J), ("offs4", offs4, J),
                             ("offs5", offs5, J), ("offs6", offs6, I)):
            lists[name] = sb.tile([P, n // LANES], U16, name=name)
            nc.sync.dma_start(lists[name][:], src)

        def part(name, lo, hi):
            return lists[name][:, lo // LANES : hi // LANES]

        f1 = sb.tile([P, T], F32)
        nc.vector.memset(f1[:], 0.0)

        q_bf = sb.tile([P, Q, PACK], BF16, align_bytes=64)
        q_view = q_raw[:].rearrange("p t q -> p q t")
        nc.vector.tensor_copy(q_bf[:, 0:88, :], q_view[:, 0:88, :])
        nc.scalar.activation(q_bf[:, 88:Q, :], q_view[:, 88:Q, :], COPY)
        q_codes = sb.tile([P, Q], U32, align_bytes=64)
        q_scales = sb.tile([P, Q], U8, align_bytes=64)
        nc.vector.quantize_mx(out=q_codes[:].bitcast(FP8X4), scales=q_scales[:],
                              in_=q_bf[:].rearrange("p q t -> p (q t)"))

        for g in range(1, 4):
            nc.vector.tensor_copy(cache_plane_i[32 * g : 32 * g + 4, 0:half], cache_plane_i[0:4, g * half : (g + 1) * half])

        b_sb = sb.tile([P, U], F32)
        for c in range(U // PIECE):
            cols = slice(c * PIECE, (c + 1) * PIECE)
            bank = psum.tile([P, PIECE], F32, name="b_bank%d" % c)
            nc.tensor.matmul_mx(out=bank[:], lhsT=q_codes[:].bitcast(FP8X4), lhsT_scale=q_scales[:],
                                rhs=draft_sb[:, 2 * cols.start : 2 * cols.stop].bitcast(FP4X4),
                                rhs_scale=draft_plane[:, cols], start=True, stop=True)
            nc.scalar.copy(b_sb[:, cols], bank[:])
        gb = sb.tile([P, I], F32)
        for lo in (0, I // 2):
            nc.scalar.activation(gb[:, lo : lo + I // 2], b_sb[:].indirect(part("offs2", lo, lo + I // 2)), COPY)

        a_sb = sb.tile([P, T], F32)
        a_banks = []
        for c in range(T // PIECE):
            cols = slice(c * PIECE, (c + 1) * PIECE)
            bank = psum.tile([P, PIECE], F32, name="a_bank%d" % c)
            nc.tensor.matmul_mx(out=bank[:], lhsT=q_codes[:].bitcast(FP8X4), lhsT_scale=q_scales[:],
                                rhs=cache_sb[c].bitcast(FP8X4),
                                rhs_scale=cache_plane[:, cols], start=True, stop=True)
            a_banks.append(bank)
            nc.vector.tensor_copy(a_sb[:, cols], bank[:])

        w = sb.tile([P, I], F32)
        for lo in (0, I // 2):
            hi = lo + I // 2
            nc.vector.tensor_tensor(w[:, lo:hi], a_sb[:].indirect(part("offs", lo, hi)), gb[:, lo:hi], SUB)

        for h in range(2):
            lo, hi = h * J // 2, (h + 1) * J // 2
            g3 = sb.tile([P, J // 2], F32, name="g3_%d" % h)
            g4 = sb.tile([P, J // 2], F32, name="g4_%d" % h)
            p1 = sb.tile([P, J // 2], F32, name="p1_%d" % h)
            nc.vector.tensor_copy(g3[:], w[:].indirect(part("offs3", lo, hi)))
            nc.scalar.activation(g4[:], w[:].indirect(part("offs4", lo, hi)), COPY)
            nc.vector.tensor_tensor(p1[:], g3[:], g4[:], MAX)
            nc.scalar.activation(f1[:].indirect(part("offs5", lo, hi)), p1[:], COPY)

        aa = sb.tile([P, T], F32)
        last = slice(T - PIECE, T)
        nc.gpsimd.tensor_tensor(aa[:, last], a_sb[:, last], f1[:, last], SUB)
        for c in range(T // PIECE - 1):
            cols = slice(c * PIECE, (c + 1) * PIECE)
            nc.vector.tensor_tensor(aa[:, cols], a_banks[c][:], f1[:, cols], SUB)

        for lo in (0, I // 2):
            hi = lo + I // 2
            y = sb.tile([P, I // 2], F32, name="y%d" % lo)
            nc.vector.tensor_tensor(y[:], aa[:].indirect(part("offs6", lo, hi)), w[:, lo:hi], ADD)
            nc.sync.dma_start(out[:, lo:hi], y[:])
